import numpy as np, ml_dtypes
CORES = [36,164,52,180,100,228,116,244]
N = 8
import mx_ref
BF = ml_dtypes.bfloat16
def gcols(t, e):
    v = np.concatenate([t.reshape(8, 16, -1, 4), np.zeros((8, 16, 1, 4), BF)], axis=2)
    return np.ascontiguousarray(np.stack([v[g][:, e[g]] for g in range(8)])).reshape(128, -1)
def tile(rs):
    return np.stack(rs, axis=2).reshape(128, -1).astype(BF)
def pick(q, e):
    c = np.concatenate([q[0].reshape(128, -1, 4), np.zeros((128, 1, 4), np.uint8)], axis=1); s = np.concatenate([q[1], np.ones((16, 1), np.uint8)], axis=1)
    return (np.ascontiguousarray(c[:, e].reshape(128, -1)), np.ascontiguousarray(s[:, e]))
def join(*qs):
    return (np.concatenate([q[0] for q in qs], axis=1), np.concatenate([q[1] for q in qs], axis=1))
def put(q, e, v):
    c, s = q[0].reshape(128, -1, 4).copy(), q[1].copy(); c[:, e] = v[0].reshape(128, -1, 4); s[:, e] = v[1]
    return (c.reshape(128, -1), s)
def pk(c, s):
    return (np.ascontiguousarray(c), mx_ref.live(s))
def emit(q):
    return q[0], q[1]
def packed(v, rng):
    q = [mx_ref.quantize(np.ascontiguousarray(v[r])) for r in range(N)]
    return np.stack([a for a, b in q]), np.stack([mx_ref.plane(b, rng) for a, b in q])
def values_of_codes():
    e, c = np.zeros((128, 128, 4), np.float32), np.zeros((128, 2, 4), np.uint8)
    e[np.arange(128), np.arange(128), 0] = 1
    c[:127, :, 0] = np.arange(256).reshape(2, 128).T[:127]
    return mx_ref.matmul(mx_ref.quantize(e.reshape(128, 512).astype(BF)), (c.reshape(128, 8), np.full((16, 2), 127, np.uint8))).T.reshape(-1).astype(np.float64)
CODE_VALUE, SCALE_VALUE = values_of_codes(), 2.0 ** (np.arange(256) - 127.0)
def decode(q):
    return (CODE_VALUE[q[0]].reshape(16, 8, -1, 4) * SCALE_VALUE[q[1]][:, None, :, None] + 0.0).reshape(128, -1).astype(np.float32)
def f(rng, *shape):
    return mx_ref.flush((rng.standard_normal(shape, dtype=np.float32) * np.exp2(rng.integers(-2, 3, shape[:-1] + (1,)))).astype(BF))
def wide(rng, *shape, cols=0):
    v = rng.standard_normal(shape, dtype=np.float32) * np.exp2(rng.integers(-12, 13, shape)).astype(np.float32)
    if cols: v *= np.repeat(np.exp2(rng.integers(-cols, cols + 1, shape[:-2] + (1, shape[-1] // 4))) * (rng.random(shape[:-2] + (1, shape[-1] // 4)) > 0.0625), 4, axis=-1).astype(np.float32)
    return mx_ref.flush(v.astype(BF))
C, E = 352, 10
def big(v):
    v = v.astype(np.float32)
    v[np.abs(v) < np.float32(2.0 ** -16)] = 0
    return v.astype(BF)
def numbers_of(rng):
    return big(f(rng, N, 128, 4 * C)), big(f(rng, N, 128, 128)), np.array(f(rng, N, 128, 512)), np.array(f(rng, N, 128, 512))
def layers(rng):
    return big(f(rng, N, 128, 2048)).reshape(N, 8, 16, 4, 8, 16, 4)
def some(rng, k):
    return np.argsort(np.argsort(rng.random((8, 32)), axis=1), axis=1) < k
def flags(rng):
    k = np.where(some(rng, E // 2), -1.0, rng.random((N, 8, 32)))
    fl = np.ones((N, 8, 32), np.int32)
    np.put_along_axis(fl, np.argsort(k, axis=2)[:, :, :E], 0, axis=2)
    return fl
def relabels(rng):
    return np.argsort(rng.random((N, 7, 32, 32)), axis=3)
def drawn(rng, x, tr, u, v, fl, w, ti=None):
    t = tr.astype(np.float32).reshape(N, 8, 16, 32, 4).copy()
    t[np.broadcast_to((fl == 0)[:, :, None, :, None], t.shape)] = 0
    if ti is None: ti = relabels(rng)
    c, p = packed(np.ascontiguousarray(w).reshape(N, 128, 2048), rng)
    return {"x": np.ascontiguousarray(x).reshape(N, 128, 4 * C).astype(BF), "tr": t.reshape(N, 128, 128).astype(BF), "u": np.ascontiguousarray(u).reshape(N, 128, 512), "v": v, "fl": fl, "ti": ti.reshape(N, 7, 1024).astype(np.int32), "wc": c, "ws": p}
def setup_inputs(rng):
    x, tr, u, v = numbers_of(rng)
    return drawn(rng, x, tr, u, v, flags(rng), layers(rng))
def setup_inputs_ties(rng):
    x, tr, u, v = numbers_of(rng)
    o = rng.permutation(N)
    x = x.reshape(N, 8, 16, C, 4)
    for r in range(N):
        a = x[r][:, :8, :24].copy()
        a[:, :, 23] = 0
        k = rng.permutation(C) % 24
        if r == o[0]: k = np.zeros(C, int)
        if r == o[1]: k = np.full(C, 23)
        x[r][:, :8] = a[:, :, k]
    u = u.reshape(N, 8, 16, 128, 4)
    for i in range(5): u[:, :, 8:, i::16] = 0
    w = layers(rng)
    w[:, :, :, :, :, :8] = 0
    return drawn(rng, x, tr, u, v, flags(rng), w)
def setup_inputs_near(rng):
    x, tr, u, v = numbers_of(rng)
    fl, ti = flags(rng), relabels(rng)
    a = int(rng.integers(N))
    fl[(a + 1) % N] = fl[a]
    o = rng.permutation(N) % 2
    x = x.astype(np.float32).reshape(N, 8, 16, C, 4)
    tr = tr.astype(np.float32).reshape(N, 8, 16, 32, 4)
    x[:, :, :8] = 0
    tr[:, :, :8] = 0
    u = u.reshape(N, 128, 128, 4)
    for i in range(5): u[:, :, i::16] = 0
    for r in range(N):
        k = 2.0 ** -30 if o[r] == 0 else 1.0
        x[r, :, :5, :, 0] = k * rng.integers(-1, 2, (8, 5, C))
        tr[r, :, :5, :, 0] = k * rng.integers(-1, 2, (8, 5, 32))
        for g in rng.permutation(8)[:4]: x[r, g, :5, rng.integers(C), 0] = 2.0 ** 27 * rng.choice([-1.0, 1.0], 5)
        for h in range(0, 128, 16):
            for i in range(5): u[r, h + i, h + i, 0] = k
    hole = np.stack([np.flatnonzero(fl[a, g] == 0) for g in range(8)])
    held = np.stack([np.flatnonzero(fl[a, g] == 1) for g in range(8)])
    n = np.arange(8 * E)
    b = held[np.arange(8)[:, None], rng.integers(0, 32 - E, (8, 8 * E))]
    b[n // E, n] = hole[n // E, n % E]
    back = np.argsort(ti[a], axis=2)
    e = b.copy()
    for g in range(8):
        for h in range(g - 1, -1, -1): e[g] = back[h, b[h], e[g]]
    bit = (e[:, None] >> np.arange(4, -1, -1)[:, None]) & 1
    j = rng.permutation(C)[:8 * E]
    s = x[a, :, :5, :, 0]
    m = np.abs(s[:, :, j])
    s[:, :, j] = np.where(bit == 1, np.maximum(m, 2.0 ** -30 if o[a] == 0 else 1.0), 0.0 - m)
    x[a, :, :5, :, 0] = s
    w = layers(rng)
    w[:, :, :8] = 0
    w[:, :, :, :, :, :8] = 0
    return drawn(rng, x, tr, u, v, fl, w, ti)
def setup_inputs_deep(rng):
    x, tr, u, v = numbers_of(rng)
    x = (rng.integers(0, 2, x.shape) * 2.0 - 1.0) * (0.8 + 0.2 * rng.random(x.shape)) * 2.0 ** 26
    tr = (rng.integers(0, 2, tr.shape) * 2.0 - 1.0) * (0.8 + 0.2 * rng.random(tr.shape)) * 2.0 ** 26
    u = (rng.integers(0, 2, u.shape) * 2.0 - 1.0) * (0.9 + 0.1 * rng.random(u.shape)) * 2.0 ** 30
    o = rng.permutation(N)
    m = some(rng, E)
    fl = np.ones((N, 8, 32), np.int32)
    for r in range(N):
        if r == o[1]: fl[r, 7][m[7]] = 0
        elif r == o[2]: fl[r, 0][m[0]] = 0
        elif r != o[0]: fl[r][m] = 0
    w = (layers(rng).astype(np.float32) * np.float32(0.0625)).astype(BF)
    return drawn(rng, x.astype(np.float32), tr.astype(np.float32), u.astype(np.float32).astype(BF), v, fl, w)
def setup_inputs_odd(rng):
    x, tr, u, v = numbers_of(rng)
    x = (1.125 + 0.25 * rng.integers(0, 4, (N, 16, 8, C, 4))) * np.exp2(-rng.integers(8, 15, (N, 16, 8, C, 4)).astype(np.float32))
    x[:, :, 0, :, 0] = 1.96875
    x = x * (rng.integers(0, 2, x.shape) * 2.0 - 1.0) * np.exp2(rng.integers(-2, 3, (N, 16, 1, C, 1)).astype(np.float32))
    return drawn(rng, x.astype(np.float32), tr, u, v, flags(rng), layers(rng))
def setup_inputs_spread(rng):
    x, tr, u, v = numbers_of(rng)
    return drawn(rng, big(wide(rng, N, 128, 4 * C, cols=6)), big(wide(rng, N, 128, 128)), u, v, flags(rng), layers(rng))
def check_inputs(d):
    b = []
    for k in ("x", "tr", "u", "v"):
        a = np.abs(d[k].astype(np.float32))
        if not (np.isfinite(a).all() and ((a == 0) | (a >= 2.0 ** -30) & (a <= 2.0 ** 30)).all()): b.append("a value of " + k)
    fl = d["fl"]
    if not ((fl == 0) | (fl == 1)).all(): b.append("a flag of fl")
    if (np.sum(fl == 0, axis=2) > E).any(): b.append("too many empty slots in a level")
    if ((d["tr"].astype(np.float32).reshape(N, 8, 16, 32, 4) != 0) & (fl == 0)[:, :, None, :, None]).any(): b.append("tr isn't zero at an empty slot")
    if (np.sort(d["ti"].reshape(N, 7, 32, 32), axis=3) != np.arange(32)).any(): b.append("ti: not the points in some order")
    none, least, most = [emit(mx_ref.quantize(np.full((128, 16), k, np.float32).astype(BF)))[1][0, 0] for k in (0.0, 2.0 ** -30, 2.0 ** 30)]
    for r in range(N):
        if ((d["wc"][r] == 0x7F) | (d["wc"][r] == 0xFF)).any(): b.append("wc: a code that is no number")
        s = mx_ref.live(d["ws"][r])
        if ((s != none) & ((s < least) | (s > most))).any(): b.append("ws: a scale out of range")
    return b
def reference(x, tr, u, v, fl, ti, wc, ws):
    qu = [mx_ref.quantize(u[r]) for r in range(N)]
    lay = [pk(wc[r], ws[r]) for r in range(N)]
    now = [x[r] for r in range(N)]
    slot = [decode(mx_ref.quantize(tr[r])).astype(BF) for r in range(N)]
    full = fl > 0
    way = np.zeros((N, 8, C), np.int64)
    for t in range(3):
        claim, came = [], []
        for r in range(N):
            q = mx_ref.quantize(now[r])
            own = decode(q)
            s = mx_ref.matmul(qu[r], q)
            e = 16 * (s[0::16] > 0) + 8 * (s[1::16] > 0) + 4 * (s[2::16] > 0) + 2 * (s[3::16] > 0) + (s[4::16] > 0)
            fail = np.full(C, 8)
            for g in range(8):
                going = fail == 8
                way[r, g] = np.where(going, e[g], -1)
                fail = np.where(going & ~full[r, g][e[g]], g, fail)
                if g < 7: e[g + 1:] = ti[r, g][32 * e[g] + e[g + 1:]]
            passed = np.where(np.arange(8)[:, None] < fail, way[r], -1)
            z = (own - gcols(slot[r], passed).astype(np.float32)).astype(BF)
            q = mx_ref.quantize(z)
            c = np.full((8, 32), C)
            j = np.flatnonzero(fail < 8)
            np.minimum.at(c, (fail[j], way[r][fail[j], j]), j)
            claim.append(c < C)
            came.append(gcols(decode(q).astype(BF), np.where(c < C, c, -1)))
            now[r] = tile([mx_ref.matmul(pick(lay[r], np.arange(128 * b, 128 * b + 128)), q) * np.float32(0.015625) + z[:, b::4].astype(np.float32) for b in range(4)])
        for r in range(N):
            take = claim[(r - 1) % N] & ~full[r]
            slot[r] = gcols(np.concatenate([slot[r], came[(r - 1) % N]], axis=1), np.arange(32) + 32 * take)
            full[r] = full[r] | take
    y, bp, rt = np.zeros((N, 128, C), np.float32), np.zeros((N, 8, C + 32), np.float32), np.zeros((N, 128, 128), np.float32)
    oc, osc = np.zeros((N, 128, 4 * C), np.uint8), np.zeros((N, 16, C), np.uint8)
    for r in range(N):
        q = mx_ref.quantize(now[r])
        y[r] = mx_ref.matmul(mx_ref.quantize(v[r]), q)
        bp[r] = np.concatenate([way[r], full[r]], axis=1)
        rt[r] = slot[r].astype(np.float32)
        oc[r], osc[r] = emit(q)
    return {"y": y, "bp": bp, "rt": rt, "oc": oc, "osc": osc}

from concourse.bass import IndirectOffsetOnAxis
from concourse.mybir import dt, AluOpType as OP, AxisListType, ActivationFunctionType

COPY = ActivationFunctionType.Copy
NV = [128, 128, 96]
PW, CAME = 160, 112
NF = 2
SMALL = {"KI": "pI1 iI1 gI1 c5I1 m7I1 cnI1 rem1 nI2 la2 lb2 lc2 ld2 le2 lf2 ma2 mb2 mc2 md2 me2 mf2",
         "KF": "iF1 gF1 c5F1 a5F1 nW2 nV2 kF8 gc8",
         "KL": "flf2 ua2 uk2 uf2 esta2 estb2 estc2 estd2 mxa1 mxb1 cnt1"}
ALIAS = {}
for _b, _s in SMALL.items():
    _k = 0
    for _n in _s.split():
        ALIAS[_n[:-1]] = (_b, _k)
        _k += int(_n[-1])
EST = ["esta", "estb", "estc", "estd"]


def _scratch():
    f, h, i, u, q, b = "float32", "bfloat16", "int32", "uint16", "float8_e4m3fn_x4", "uint8"
    s = {"tabd": ("dram", [1, 7424], h), "fdr0": ("dram", [128, 2], h), "fdr1": ("dram", [128, 2], h)}
    for d, names in ((i, "KI:40 zix:2 tic:64 t32:2048 flI:2"),
                     (f, "KF:32 KL:32 pF:1 tt:128 dd:128 ge:128 eq:128 qa:128 qb:128 qc:128 qd:128 ix:128 rel:112 wa:112 wb:112 wc1:112 MB:112 wt:352 of1:24 "
                         "jk:352 MV:352 RT:128 BPO:352 FO:2 YO:384"),
                     (u, "R1:2 R2:2 UP:8 OF:192 OC:24 L:32 CL:2 UL:2 UL3:4"),
                     (h, "MS:128 MC:128 hd:128 WM:112 WN:112 r64:8 ET:2048 tib:64 TAB:7424 flc:2 UT:512 VT:512 TT:512 ZT:512 XT:1536 AB:384 SC:3456 GO0:128 GO1:128 GO2:128 "
                         "CO:384 DS:32 AM:64 FP:768 TG:768 ZS:1536 ZP:1536 TV0:640 TV1:640 TV2:640 CT1:256 CT2:256 CB:256 crow:256 CLT:512 "
                         "w_0:2 w_1:2 w_2:2 fw0:2 fw1:2 fw2:2")):
        for n in names.split():
            n, w = n.split(":")
            s[n] = ("sbuf", [128, int(w)], d)
    for n in "EQ:512 QU:128 QP:128 QV:128 QT:128 WC:512 QO:128 QX:384 QZ:384 CQ0:128 CQ1:128 CQ2:128 LC:192".split():
        n, w = n.split(":")
        s[n] = ("sbuf", [128, int(w)], q)
        s[n + "s"] = ("sbuf", [128, int(w)], b)
    for n, w in (("psS", 1024), ("psF", 1024), ("psR", 2048)):
        s[n] = ("psum", [128, w], f)
    return s


SCRATCH = _scratch()
SEMAPHORES = ["sV", "sS", "sT", "sG", "sent", "rf0", "rf1", "rf2", "rc0", "rc1", "rc2"] + ["d%d" % k for k in range(60)]
PLAN = {}
WAKE, DMALAT, NETLAT, CYC = 0.1, 2.0, 3.0, 0.00083


def bits(v):
    n, a, b, st = v[:4]
    if n in ALIAS:
        n, o = ALIAS[n]
        a, b = a + o, b + o
    if n[:2] == "ps":
        a, b, st = a - a % 512, a - a % 512 + 512, 1
    return (n, ((1 << (b - a)) - 1) << a if st == 1 else sum(1 << k for k in range(a, b, st)))


def plan(ops):
    hist, deps, n = {}, [], len(ops)
    for k, o in enumerate(ops):
        d = set()
        acc = [bits(v) + (False,) for v in o["R"]] + [bits(v) + (True,) for v in o["W"]]
        for buf, m, w in acc:
            d.update(k2 for m2, k2, w2 in hist.get(buf, ()) if (w or w2) and m & m2)
        for buf, m, w in acc:
            hist.setdefault(buf, []).append((m, k, w))
        deps.append(sorted(d))
    succ = [[] for _ in ops]
    for k in range(n):
        for j in deps[k]: succ[j].append(k)
    prio = [0.0] * n
    for k in range(n - 1, -1, -1):
        prio[k] = min(ops[k]["dur"].values()) + ops[k]["lat"] + max([prio[j] for j in succ[k]] + [0.0])
    left = [len(d) for d in deps]
    ready = {k: 0.0 for k in range(n) if not left[k]}
    avail, fin, order = {}, [0.0] * n, []
    while ready:
        opts = []
        for k, r in ready.items():
            end, st, q = min((max(r, avail.get(q, 0.0)) + du, max(r, avail.get(q, 0.0)), q) for q, du in ops[k]["dur"].items())
            opts.append((st, -prio[k] - ops[k]["boost"], k, q, end))
        lo = min(opts)[0] + 0.03
        st, _, k, q, end = min((o for o in opts if o[0] <= lo), key=lambda o: o[1])
        del ready[k]
        avail[q] = end
        fin[k] = end + ops[k]["lat"]
        order.append((k, q, st))
        for j in succ[k]:
            left[j] -= 1
            if not left[j]: ready[j] = max(fin[i] for i in deps[j])
    return order, deps, max(fin)


def build(g, core, T, topo, nxt):
    ops = []

    def ap(v):
        n, a, b, st = v[:4]
        if n in ALIAS:
            n, o = ALIAS[n]
            a, b = a + o, b + o
        r = T[n][:, a:b] if st == 1 else T[n][:, a:b:st]
        if len(v) > 4 and v[4] == "c": return r.bitcast(dt.uint8)
        return r.indirect(ap(v[4])) if len(v) > 4 else r

    def vw(n, a, b=None, st=1):
        return (n, a, a + 1 if b is None else b, st)

    def ind(v, *off):
        return v + (vw(*off),)

    def add(dur, fn, ins, outs, lat=WAKE, kind="c", nd=0, boost=0.0):
        R = [v[:4] for v in ins] + [v[4][:4] for v in ins if len(v) > 4 and v[4] != "c"]
        ops.append({"dur": dur, "fn": fn, "R": R, "W": [v[:4] for v in outs], "lat": lat, "kind": kind, "nd": nd, "boost": boost})

    def cost(v, k):
        n = len(range(v[1], v[2], v[3]))
        return n, max(64, n * k) * CYC

    def isind(*vs):
        return any(len(v) > 4 and v[4] != "c" for v in vs)

    def ts(out, in0, s1, s2, op0, op1=None):
        n, d = cost(out, 1.0)
        sc = [s for s in (s1, s2) if isinstance(s, tuple)]
        if isind(in0): d = 0.05 + n * 1.5 * CYC
        val = lambda s: ap(s) if isinstance(s, tuple) else s
        if op1 is None: fn = lambda: g.vector.tensor_scalar(ap(out), ap(in0), val(s1), None, op0)
        else: fn = lambda: g.vector.tensor_scalar(ap(out), ap(in0), val(s1), val(s2), op0, op1)
        add({"V": d}, {"V": fn}, [in0] + sc, [out])

    def tt(out, a, b, op):
        n, d = cost(out, 1.0 if a[0][:2] == "ps" else 2.0)
        if isind(a): d = 0.05 + n * 1.5 * CYC
        add({"V": d}, {"V": lambda: g.vector.tensor_tensor(ap(out), ap(a), ap(b), op)}, [a, b], [out])

    def cp(out, a, q="V", scale=1.0, acc=None):
        n, d = cost(out, 1.0)
        i = isind(a)
        kw = {}
        if scale != 1.0: kw["scale"] = scale
        fns = {"V": lambda: g.vector.tensor_copy(ap(out), ap(a)),
               "S": lambda: g.scalar.activation(ap(out), ap(a), COPY, accum_out=ap(acc)) if acc else g.scalar.activation(ap(out), ap(a), COPY, **kw)}
        durs = {"V": 0.05 + n * 1.5 * CYC if i else d, "S": 0.065 + n * 1.5 * CYC if i else d}
        add({k: durs[k] for k in q}, {k: fns[k] for k in q}, [a], [out] + ([acc] if acc else []))

    def scan(out, d0, d1, init, op0, op1):
        add({"V": cost(out, 0.5)[1]}, {"V": lambda: g.vector.tensor_tensor_scan(ap(out), ap(d0), ap(d1), init, op0, op1)}, [d0, d1], [out])

    def fill(out, val):
        add({"V": cost(out, 0.5)[1]}, {"V": lambda: g.vector.memset(ap(out), val)}, [], [out])

    def quant(q, a, t, ta, n=128):
        c, s, i = vw(q, a, a + n), vw(q + "s", a, a + n), vw(t, ta, ta + 4 * n)
        add({"V": 0.012 + 0.88e-3 * n}, {"V": lambda: g.vector.quantize_mx(ap(c), ap(s), ap(i))}, [i], [c, s])

    def mm(ps, pa, lq, la, rq, ra, n=128):
        o = vw(ps, pa, pa + n)
        i = [vw(lq, la, la + 128), vw(lq + "s", la, la + 128), vw(rq, ra, ra + n), vw(rq + "s", ra, ra + n)]
        add({"T": (n + 16) * 0.00085}, {"T": lambda: g.tensor.matmul_mx(ap(o), ap(i[0]), ap(i[1]), ap(i[2]), ap(i[3]), True, True)}, i, [o])

    def iota(out, pattern, base, cm, small=True):
        kw = {"allow_small_or_imprecise_dtypes": True} if small else {}
        add({"G": 0.13 + cost(out, 2.0)[0] * 2 * CYC}, {"G": lambda: g.iota(ap(out), pattern, base, cm, **kw)}, [], [out])

    def ld(q, pairs, ins, outs, nd=1, boost=0.0):
        add({q: 0.06 * nd}, {q: lambda: [(g.sync if q == "Y" else g.scalar).dma_start(o, i) for o, i in pairs()]}, ins, outs, DMALAT, "d", nd, boost)

    def rows(out, src, dep, col, last, lat, boost=0.0):
        ix = vw("zix", col)
        add({"G": 1.7}, {"G": lambda: g.indirect_dma_start(ap(out), None, T[src][:], IndirectOffsetOnAxis(ap=ap(ix), axis=0), bounds_check=last)}, [ix] + dep, [out], lat, "d", 1, boost)

    def send(out, in_, sem, boost=0.0):
        ne = 8 if T is None else len(topo.engines(core, nxt))
        def fn():
            rid, pid = topo.addr(nxt, core)
            g.remote_dma(ap(out) if out[0][:3] != "fdr" else T[out[0]][:], ap(in_), T.sem[sem], T.sem.sent, pid, rid, topo.mask(core, nxt))
        add({"G": 0.3}, {"G": fn}, [in_], [out], NETLAT, "n", (sem, ne), boost)

    iota(vw("zix", 0, 2), [[1, 2]], 0, 0, False)
    iota(vw("pI", 0), [[0, 1]], 0, 1, False)
    ld("Y", lambda: [(T.tic[0:112, :], T.ti[:])], [], [vw("tic", 0, 64)], boost=50.0)
    ld("S", lambda: [(T.UT[:], T.u[:])], [], [vw("UT", 0, 512)], boost=40.0)
    for c in range(3):
        v = vw("XT", 512 * c, 512 * c + 4 * NV[c])
        ld("YSY"[c], lambda v=v: [(ap(v), T.x[:, v[1]:v[2]])], [], [v], boost=45.0 - c)
    ld("S", lambda: [(T.flI[:], T.fl[:])], [], [vw("flI", 0, 2)], boost=38.0)
    for l in range(2): rows(vw("t32", 1024 * l, 1024 * l + 1024), "ti", [], l, 6, 3.5, boost=50.0)
    for o, i, s, op in (("iI", "pI", 15, OP.bitwise_and), ("gI", "pI", 4, OP.arith_shift_right), ("a5F", "pI", 5.0, OP.add)):
        ts(vw(o, 0), vw(i, 0), s, None, op)
    cp(vw("c5I", 0), vw("a5F", 0))
    ts(vw("m7I", 0), vw("c5I", 0), 15, None, OP.bitwise_and)
    for o, i in (("pF", "pI"), ("iF", "iI"), ("gF", "gI"), ("c5F", "m7I")): cp(vw(o, 0), vw(i, 0))
    iota(vw("kF", 0, 8), [[16, 8]], 0, 0)
    iota(vw("tt", 0, 128), [[0, 8], [1, 16]], 0, 0)
    iota(vw("ix", 0, 128), [[1, 128]], 0, 0)
    iota(vw("gc", 0, 8), [[1024, 8]], -32, 0)
    iF, gF = vw("iF", 0), vw("gF", 0)
    full = lambda n, w=128: vw(n, 0, w)
    ts(full("UP", 8), full("kF", 8), vw("c5F", 0), None, OP.add)
    quant("QU", 0, "UT", 0)
    for s, d in (("QU", "QP"), ("QUs", "QPs")):
        fn = (lambda: g.vector.tensor_copy(T.QP[:].bitcast(dt.uint32), T.QU[:].bitcast(dt.uint32).indirect(T.UP[:, 0:8]))) if s == "QU" else \
             (lambda: g.vector.tensor_copy(T.QPs[:], T.QUs[:].indirect(T.UP[:, 0:8])))
        add({"V": 0.2}, {"V": fn}, [full(s), full("UP", 8)], [full(d)])
    ts(full("hd"), full("tt"), 12.0, 2.0, OP.is_ge, OP.mult)
    add({"V": 0.06}, {"V": lambda: g.vector.tensor_scalar(T.tib[0:112, :], T.tic[0:112, :], 1.0, -1.0, OP.add, OP.mult)}, [full("tic", 64)], [full("tib", 64)])
    ts(full("nW", 2), full("kF", 2), iF, None, OP.add)
    ts(full("flf", 2), full("flI", 2), -33.0, -127.0, OP.mult, OP.add)
    tt(full("flc", 2), full("flf", 2), full("nW", 2), OP.add)
    ts(full(EST[0], 2), full("flI", 2), 0.0, float(CAME), OP.is_equal, OP.mult)
    ld("Y", lambda: [(T.tabd[0:1, 0:7168], T.tib[0:112, :])], [full("tib", 64)], [vw("tabd", 0, 7168)])
    ld("Y", lambda: [(T.tabd[0:1, 7168:7424], T.flc[:])], [full("flc", 2)], [vw("tabd", 7168, 7424)])
    rows(full("TAB", 7424), "tabd", [full("tabd", 7424)], 0, 0, 5.0)
    ts(full("dd"), full("tt"), iF, None, OP.subtract)
    ts(full("ge"), full("dd"), 0.0, None, OP.is_ge)
    ts(full("qa"), full("dd"), 0.0, 31.0, OP.is_equal, OP.mult)
    tt(full("qb"), full("ge"), full("qa"), OP.add)
    ts(vw("eq", 0, 16), vw("tt", 0, 16), 15.0, -2.0, OP.is_equal, OP.mult)
    ts(vw("eq", 16, 128), vw("tt", 16, 128), 15.0, -33.0 / 32.0, OP.is_equal, OP.mult)
    ts(full("qc"), full("eq"), 1.0, None, OP.add)
    tt(full("MS"), full("qb"), full("qc"), OP.mult)
    fill(full("ET", 2048), 0.0)
    for k in range(4):
        ts(vw("ET", 513 * k, 512 * k + 512, 4), full("ix"), vw("pF", 0), 0.015625, OP.is_equal, OP.mult)
        quant("EQ", 128 * k, "ET", 512 * k)
    ts(full("qa"), full("ge"), -128.0, 128.0, OP.mult, OP.add)
    ts(full("qb"), full("dd"), 0.0, -64.0, OP.is_equal, OP.mult)
    ts(full("qc"), full("tt"), 15.0, 192.0, OP.is_equal, OP.mult)
    tt(full("qd"), full("qa"), full("qb"), OP.add)
    tt(full("MC"), full("qd"), full("qc"), OP.add)
    fill(full("r64", 8), 64.0)
    fill(full("AM", 64), 0.0)
    fill(vw("XT", 1408, 1536), 0.0)
    fill(vw("ZS", 1408, 1536), 0.0)
    for k in range(4): fill(vw("ZP", 384 * k + 352, 384 * k + 384), 0.0)
    fill(vw("TT", 128, 512), 0.0)
    ld("S", lambda: [(T.TT[:, 0:128], T.tr[:])], [], [full("TT")], boost=20.0)
    quant("QT", 0, "TT", 0)
    for t in range(3): fill(full("TV%d" % t, 640), 0.0)
    for k in range(4):
        b = 512 * (k % 2)
        mm("psF", b, "EQ", 128 * k, "QT", 0)
        for s in range(2): cp(vw("TV0", PW * k + 16 * s, PW * k + 16 * s + 16), vw("psF", b + s, b + 32, 2), "S", -1.0)
    two = lambda n: vw(n, 0, 2)
    cp(two("nI"), two("nW"))
    for o, i, s, s2, op, op2 in (("la", "nI", 11.0, None, OP.mult, None), ("lb", "la", 5, None, OP.arith_shift_right, None), ("lc", "lb", -24.0, None, OP.mult, None),
                                 ("ld", "lb", gF, None, OP.add, None), ("le", "ld", 7, None, OP.bitwise_and, None), ("lf", "nI", 8.0, None, OP.mult, None)):
        ts(two(o), two(i), s, s2, op, op2)
    tt(two("la"), two("lc"), two("lf"), OP.add)
    tt(two("ld"), two("la"), two("le"), OP.add)
    cp(two("R1"), two("ld"))
    for o, i, s, s2, op, op2 in (("ma", "nI", 3, None, OP.arith_shift_right, None), ("mb", "nI", 7, None, OP.bitwise_and, None), ("mc", "mb", -1.0, gF, OP.mult, OP.add),
                                 ("md", "mc", 8.0, None, OP.add, None), ("me", "md", 7, None, OP.bitwise_and, None), ("mf", "me", 0.0, 32.0, OP.is_gt, OP.mult),
                                 ("mb", "me", 3.0, None, OP.mult, None)):
        ts(two(o), two(i), s, s2, op, op2)
    tt(two("mc"), two("mb"), two("ma"), OP.add)
    tt(two("md"), two("mc"), two("mf"), OP.add)
    cp(two("R2"), two("md"))
    ts(full("rel", 112), full("ix", 112), iF, -33.0, OP.subtract, OP.add)
    ts(full("wa", 112), full("rel", 112), 0.0, None, OP.is_equal)
    ts(full("wb", 112), full("rel", 112), 16.0, None, OP.is_equal)
    ts(full("wc1", 112), full("rel", 112), 16.0, 1024.0, OP.is_equal, OP.mult)
    tt(full("WM", 112), full("wa", 112), full("wb", 112), OP.subtract)
    tt(full("WN", 112), full("wa", 112), full("wc1", 112), OP.add)
    iota(full("wt", 352), [[-1, 352]], 352, 0)
    ts(two("nV"), two("nW"), -160.0, None, OP.add)
    fill(vw("CLT", 128, 512), 0.0)
    fill(full("ZT", 512), 0.0)
    quant("QO", 0, "ZT", 0)
    ld("Y", lambda: [(T.LC[:, 32:128].bitcast(dt.uint8), T.QO[:, 0:96].bitcast(dt.uint8))], [full("QO", 96)], [vw("LC", 32, 128)])
    ld("Y", lambda: [(T.LCs[:, 32:128], T.QOs[:, 0:96])], [full("QOs", 96)], [vw("LCs", 32, 128)])
    ld("Y", lambda: [(T.WC[:].bitcast(dt.uint8), T.wc[:])], [], [full("WC", 512)])
    ld("S", lambda: [(T.WCs[:], T.ws[:])], [], [full("WCs", 512)])
    fill(full("MB", 112), -1.0)
    for a in (0, 33): iota(vw("MB", a, a + 32), [[1, 2], [2, 16]], 0, 0)
    ld("S", lambda: [(T.VT[:], T.v[:])], [], [full("VT", 512)])
    quant("QV", 0, "VT", 0)

    ctn, cta = "TAB", 7168
    for t in range(3):
        for c in range(3):
            quant("QX", 128 * c, "XT", 512 * c)
            b, s0 = 512 * (c % 2), 1152 * c
            mm("psS", b, "QX", 128 * c, "QP", 0)
            ab = vw("AB", 128 * c, 128 * c + 128)
            ts(ab, vw("psS", b, b + 128), 0.0, None, OP.is_gt)
            scan(vw("SC", s0, s0 + 128), full("hd"), ab, 0.0, OP.mult, OP.add)
            ts(vw("SC", s0 + 15), vw("SC", s0 + 15), 32.0, 32.0, OP.mult, OP.add)
        for l in range(7):
            for c in range(3):
                s0, n, o0, go = 1152 * c, 7 - l, 64 * c + 8 * l, "GO%d" % c
                ts(vw("OF", o0, o0 + n), vw("SC", s0 + 144 * l + 31, s0 + 128 * l + 128, 16), vw("SC", s0 + 144 * l + 15), -32.0 if l == 0 else -33.0, OP.add, OP.add)
                gout = full(go, 16 * n)
                if t == 0 and l < 2: ts(gout, ind(vw("t32", 1024 * l, 1024 * l + 1024), "OF", o0, o0 + n), 1.0, -1.0, OP.add, OP.mult)
                else: cp(gout, ind(vw("TAB", 1024 * l, 1024 * l + 1024), "OF", o0, o0 + n), "VS")
                scan(vw("SC", s0 + 144 * (l + 1), s0 + 128 * (l + 2)), gout, full("MS", 16 * n), 0.0, OP.min, OP.mult)
        for k in range(NF):
            mm("psF", 512 * (k % 2), "EQ", 128 * k, "QX", 0, 384)
            cp(vw("FP", 384 * k, 384 * k + 352), vw("psF", 512 * (k % 2), 512 * (k % 2) + 352), "S")
        if t:
            fd, nn = "fdr%d" % (t - 1), "CT%d" % t
            ld("Y", lambda fd=fd: [(T.crow[0:1, :], T[fd][:])], [two(fd)], [full("crow", 256)])
            add({"G": 1.0}, {"G": lambda: g.partition_broadcast(T.CB[:], T.crow[0:1, :], 128)}, [full("crow", 256)], [full("CB", 256)])
            tt(full(nn, 256), vw(ctn, cta, cta + 256), full("CB", 256), OP.min)
            ctn, cta = nn, 0
        for c in range(3):
            s0, c8, go = 1152 * c, vw("of1", 8 * c, 8 * c + 8), "GO%d" % c
            tt(c8, vw("SC", s0 + 15, s0 + 1024, 144), full("gc", 8), OP.add)
            ts(vw("OC", 8 * c, 8 * c + 8), c8, 0.03125, None, OP.mult)
            cp(full(go), ind(vw(ctn, cta, cta + 256), "OC", 8 * c, 8 * c + 8), "VS")
            scan(vw("CO", 128 * c, 128 * c + 128), full(go), full("MC"), 0.0, OP.min, OP.add)
            scan(vw("DS", 8 * c, 8 * c + 8), full("r64", 8), vw("CO", 128 * c + 15, 128 * c + 128, 16), -1.0, OP.mult, OP.max)
        ts(full("AM", 32), ind(full("DS", 24), "R1", 0, 2), 64.0, 32.0, OP.min, OP.add)
        for q, ds in (("Y", [1, 2, 3, 4]), ("S", [5, 6, 7])):
            def turn(ds=ds):
                r = []
                for d in ds:
                    a, b = 32 + 3 * d, 35 + 3 * d
                    r += [(T.AM[16 * d:128, a:b], T.AM[0:128 - 16 * d, 3 * d:3 * d + 3]), (T.AM[0:16 * d, a:b], T.AM[128 - 16 * d:128, 3 * d:3 * d + 3])]
                return r
            ld(q, turn, [full("AM", 32)], [vw("AM", 32 + 3 * d, 35 + 3 * d) for d in ds], 2 * len(ds))
        cp(full("L", 32), ind(full("AM", 64), "R2", 0, 2))

        lall = ("L", 0, 22)
        cp(full("jk", 352), ind(full("WN", 112), *lall), "S", acc=vw("cnt", 0))
        cp(vw("cnI", 0), vw("cnt", 0))
        ts(vw("rem", 0), vw("cnI", 0), 1023, None, OP.bitwise_and)
        wn = "w_%d" % t
        ts(vw(wn, 0), vw("rem", 0), 0.0, vw("nV", 0), OP.is_gt, OP.mult)
        ts(vw(wn, 1), vw("cnt", 0), 1024.0, vw("nV", 1), OP.is_ge, OP.mult)
        fland, fw = "fdr%d" % t if t < 2 else "fw2", "fw%d" % t
        send(two(fland), two(wn), "rf%d" % t, boost=5.0)

        tv = "TV%d" % t
        for c in range(3):
            n, j = NV[c], 128 * c
            for k in range(4):
                z, b = vw("ZS", 512 * c + k, 512 * c + 4 * n, 4), 512 * (k % 2)
                pick = ind(vw(tv, PW * k, PW * k + CAME), "L", 8 * c, 8 * c + n // 16)
                if k < NF: tt(z, pick, vw("FP", 384 * k + j, 384 * k + j + n), OP.add)
                else:
                    tg = vw("TG", 384 * (k - NF) + j, 384 * (k - NF) + j + n)
                    mm("psF", b, "EQ", 128 * k, "QX", j)
                    cp(tg, pick, "S")
                    tt(z, vw("psF", b, b + n), tg, OP.add)
                cp(vw("ZP", 384 * k + j, 384 * k + j + n), z, "S", 64.0)
            quant("QZ", j, "ZS", 512 * c)
            for k in range(4):
                mm("psR", 512 * k, "WC", 128 * k, "QZ", j)
                tt(vw("XT", 512 * c + k, 512 * c + 4 * n, 4), vw("psR", 512 * k, 512 * k + n), vw("ZP", 384 * k + j, 384 * k + j + n), OP.add)

        tt(full("MV", 352), ind(full("WM", 112), *lall), full("wt", 352), OP.mult)
        for nm, op, sg, s in (("mxa", OP.max, -1.0, 0), ("mxb", OP.min, 1.0, 1)):
            add({"V": 352 * CYC}, {"V": lambda nm=nm, op=op: g.vector.tensor_reduce(ap(vw(nm, 0)), T.MV[:], AxisListType.X, op)}, [full("MV", 352)], [vw(nm, 0)])
            ts(vw("CL", s), vw(nm, 0), sg, 352.0, OP.mult, OP.add)
        for k in range(4): cp(vw("CLT", k, 128, 4), ind(vw("ZP", 384 * k, 384 * k + 384), "CL", 0, 2), "S")
        cq, la = "CQ%d" % t, (0, 128, 160)[t]
        quant(cq, 0, "CLT", 0)
        send(vw("LC", la, la + 32) + ("c",), vw(cq, 0, 32) + ("c",), "rc%d" % t)
        send(vw("LCs", la, la + 32), vw(cq + "s", 0, 32), "rc%d" % t)

        if t < 2: ld("Y", lambda fw=fw, fl=fland: [(T[fw][:], T[fl][:])], [two(fland)], [two(fw)])
        ts(two("ua"), two(fw), 0.0, float(CAME), OP.is_lt, OP.mult)
        tt(two("uk"), two("ua"), two(EST[t]), OP.min)
        tt(two("uf"), two("uk"), two("nW"), OP.add)
        tt(two(EST[t + 1]), two(EST[t]), two("uk"), OP.subtract)
        if t < 2: cp(two("UL"), two("uf"))
        else:
            for s in range(2): cp(vw("UL3", 2 * s), vw("uf", s))
        lv, off = ((0, 0), (32, 96), (64, 96))[t]
        for k in range(4):
            b = 512 * (k % 2)
            mm("psF", b, "EQ", 128 * k, "LC", lv)
            cp(vw(tv, PW * k + CAME, PW * k + CAME + 32), vw("psF", b + off, b + off + 32), "S", -1.0)
            win = vw(tv, PW * k, PW * k + CAME + 32)
            if t < 2: cp(vw("TV%d" % (t + 1), PW * k, PW * k + 32), ind(win, "UL", 0, 2), "S")
            else:
                for s in range(2): cp(vw("RT", 4 * s + k, 128, 8), ind(win, "UL3", 2 * s, 2 * s + 1), "S", -64.0)

    cp(full("BPO", 352), ind(full("MB", 112), "L", 0, 22), "S")
    ld("Y", lambda: [(T.bp[:, 0:352], T.BPO[0:128:16, :])], [full("BPO", 352)], [])
    ts(two("FO"), two(EST[3]), 0.0, None, OP.is_equal)
    ld("Y", lambda: [(T.bp[:, 352:384], T.FO[:])], [two("FO")], [])
    ld("Y", lambda: [(T.rt[:], T.RT[:])], [full("RT")], [])
    for c in range(3):
        n, j, b = NV[c], 128 * c, 512 * (c % 2)
        quant("QX", j, "XT", 512 * c)
        mm("psS", b, "QV", 0, "QX", j)
        cp(vw("YO", j, j + n), vw("psS", b, b + n))
        ld("Y", lambda j=j, n=n: [(T.y[:, j:j + n], T.YO[:, j:j + n])], [vw("YO", j, j + n)], [])
        ld("S", lambda j=j, n=n: [(T.oc[:, 4 * j:4 * j + 4 * n], T.QX[:, j:j + n].bitcast(dt.uint8))], [vw("QX", j, j + n)], [])
    ld("S", lambda: [(T.osc[4 * k:4 * k + 4, :], T.QXs[32 * k:32 * k + 4, 0:352]) for k in range(4)], [full("QXs", 352)], [], 4)
    return ops


def rank_program(g, core, T, topo):
    rank = T.rank_of(core)
    if rank is None: return
    ops = build(g, core, T, topo, T.cores[(rank + 1) % len(T.cores)])
    if "o" not in PLAN: PLAN["o"] = plan(ops)
    order, deps, _ = PLAN["o"]
    eng = {"V": g.vector, "S": g.scalar, "T": g.tensor, "G": g, "Y": g.sync}
    cnt, done, snap, know, nd = {}, {}, {}, {q: {} for q in eng}, 0
    for k, q, _ in order:
        o, kn = ops[k], know[q]
        for (s, v), d in sorted(((done[d], d) for d in deps[k]), key=lambda x: -x[0][1]):
            if kn.get(s, 0) < v:
                eng[q].wait_ge(T.sem[s], v)
                for s2, v2 in list(snap[d].items()) + [(s, v)]: kn[s2] = max(kn.get(s2, 0), v2)
        r = o["fn"][q]()
        if o["kind"] == "c":
            s = "s" + q
            cnt[s] = cnt.get(s, 0) + 1
            r.then_inc(T.sem[s], 1)
        elif o["kind"] == "d":
            s = "d%d" % nd
            nd += 1
            for i in (r if isinstance(r, list) else [r]): i.then_inc(T.sem[s], 16)
            cnt[s] = 16 * o["nd"]
        else:
            s, ne = o["nd"]
            cnt[s] = cnt.get(s, 0) + ne
            cnt["sent"] = cnt.get("sent", 0) + ne
        done[k] = (s, cnt[s])
        snap[k] = dict(kn) if o["kind"] != "n" else {}
    for s in sorted(cnt):
        if know["G"].get(s, 0) < cnt[s]: g.wait_ge(T.sem[s], cnt[s])
